import numpy as np, ml_dtypes
CORES = [0,1,2,3,4,5,6,7]
N = 8
def setup_inputs(rng):
    return {"x": rng.standard_normal((N, 128, 8), dtype=np.float32).astype(ml_dtypes.bfloat16)}
def reference(x):
    s = np.maximum.accumulate(x, axis=0)
    y = np.full(x.shape, np.nan, x.dtype)
    y[1:] = s[:-1]
    return {"y": y}

@@ -1,0 +1,50 @@
+from concourse.bass import DstId, RemoteDMATransfer
+
+N = 8
+FOLDER = 0
+
+SCRATCH = {
+    "gath": ("dram", [N - 1, 128, 8], "bfloat16"),
+    "land": ("dram", [128, 8], "bfloat16"),
+}
+SEMAPHORES = ["ready", "left", "result", "stored"]
+
+SEND_MASK, SEND_ENGINES = 0x000F, 4
+FOLD_ENGINES = 2
+
+
+def rank_program(g, core, T, topo):
+    rank = T.rank_of(core)
+    if rank is None:
+        return
+    sem = T.sem
+
+    if rank == FOLDER:
+        g.sync.dma_start(T.gath[rank], T.x[:]).then_inc(sem.ready, 16)
+        g.wait_ge(sem.ready, 16 + (N - 2) * SEND_ENGINES)
+        transfers = []
+        for r in range(1, N):
+            rid, pid, _se = topo.addr(T.cores[r])
+            mask = 0b11 << (FOLD_ENGINES * (r - 1))
+            if r == 1:
+                transfers.append(RemoteDMATransfer(
+                    dst_ids=[DstId(rid=rid, pnc=pid)], dma_engine_mask=mask, remote_sem=sem.result,
+                    src=T.gath[0], dst=T.land[:], alu_op=0))
+            else:
+                transfers.append(RemoteDMATransfer(
+                    dst_ids=[DstId(rid=rid, pnc=pid)], dma_engine_mask=mask, remote_sem=sem.result,
+                    srcs=[T.gath[i] for i in range(r)], dsts=[T.land[:]], alu_op=2))
+        g.remote_dma_fused(transfers, local_sem=sem.left)
+        g.wait_ge(sem.left, (N - 1) * FOLD_ENGINES)
+        return
+
+    if rank < N - 1:
+        g.sync.dma_start(T.gath[rank], T.x[:]).then_inc(sem.ready, 16)
+        g.wait_ge(sem.ready, 16)
+        rid, pid, _se = topo.addr(T.cores[FOLDER])
+        g.remote_dma(T.gath[rank], T.gath[rank], sem.ready, sem.left, pid, rid, SEND_MASK)
+        g.wait_ge(sem.left, SEND_ENGINES)
+
+    g.sync.wait_ge(sem.result, FOLD_ENGINES)
+    g.sync.dma_start(T.y[:], T.land[:]).then_inc(sem.stored, 16)
+    g.sync.wait_ge(sem.stored, 16)

@@ -1,16 +1,14 @@
 from concourse.bass import DstId, RemoteDMATransfer
 
 N = 8
-FOLDER = 0
+FOLDS = {0: (5, 6, 7), 1: (2, 3, 4)}
+ENGINES = 4
 
 SCRATCH = {
     "gath": ("dram", [N - 1, 128, 8], "bfloat16"),
     "land": ("dram", [128, 8], "bfloat16"),
 }
-SEMAPHORES = ["ready", "left", "result", "stored"]
-
-SEND_MASK, SEND_ENGINES = 0x000F, 4
-FOLD_ENGINES = 2
+SEMAPHORES = ["staged", "gathered", "result", "left", "stored"]
 
 
 def rank_program(g, core, T, topo):
@@ -19,32 +17,38 @@ def rank_program(g, core, T, topo):
         return
     sem = T.sem
 
-    if rank == FOLDER:
-        g.sync.dma_start(T.gath[rank], T.x[:]).then_inc(sem.ready, 16)
-        g.wait_ge(sem.ready, 16 + (N - 2) * SEND_ENGINES)
-        transfers = []
-        for r in range(1, N):
-            rid, pid, _se = topo.addr(T.cores[r])
-            mask = 0b11 << (FOLD_ENGINES * (r - 1))
-            if r == 1:
-                transfers.append(RemoteDMATransfer(
-                    dst_ids=[DstId(rid=rid, pnc=pid)], dma_engine_mask=mask, remote_sem=sem.result,
-                    src=T.gath[0], dst=T.land[:], alu_op=0))
-            else:
-                transfers.append(RemoteDMATransfer(
-                    dst_ids=[DstId(rid=rid, pnc=pid)], dma_engine_mask=mask, remote_sem=sem.result,
-                    srcs=[T.gath[i] for i in range(r)], dsts=[T.land[:]], alu_op=2))
-        g.remote_dma_fused(transfers, local_sem=sem.left)
-        g.wait_ge(sem.left, (N - 1) * FOLD_ENGINES)
-        return
+    def dst_id(r):
+        rid, pid, _se = topo.addr(T.cores[r])
+        return DstId(rid=rid, pnc=pid)
+
+    left = 0
 
     if rank < N - 1:
-        g.sync.dma_start(T.gath[rank], T.x[:]).then_inc(sem.ready, 16)
-        g.wait_ge(sem.ready, 16)
-        rid, pid, _se = topo.addr(T.cores[FOLDER])
-        g.remote_dma(T.gath[rank], T.gath[rank], sem.ready, sem.left, pid, rid, SEND_MASK)
-        g.wait_ge(sem.left, SEND_ENGINES)
+        g.sync.dma_start(T.gath[rank], T.x[:]).then_inc(sem.staged, 16)
+        g.wait_ge(sem.staged, 16)
+        takers = [f for f in sorted(FOLDS) if f != rank and max(FOLDS[f]) > rank]
+        g.remote_dma_fused([RemoteDMATransfer(
+            dst_ids=[dst_id(f) for f in takers], dma_engine_mask=0x000F,
+            remote_sem=sem.result if rank == 0 else sem.gathered,
+            srcs=[T.gath[rank]], dsts=[T.gath[rank] for _f in takers], alu_op=0)], local_sem=sem.left)
+        left += ENGINES
 
-    g.sync.wait_ge(sem.result, FOLD_ENGINES)
-    g.sync.dma_start(T.y[:], T.land[:]).then_inc(sem.stored, 16)
-    g.sync.wait_ge(sem.stored, 16)
+    if rank in FOLDS:
+        foreign = max(FOLDS[rank]) - 1
+        if rank == 1:
+            g.wait_ge(sem.result, ENGINES)
+            foreign -= 1
+        g.wait_ge(sem.gathered, foreign * ENGINES)
+        g.remote_dma_fused([RemoteDMATransfer(
+            dst_ids=[dst_id(r)], dma_engine_mask=0x000F << (ENGINES * k), remote_sem=sem.result,
+            srcs=[T.gath[i] for i in range(r)], dsts=[T.land[:]], alu_op=2)
+            for k, r in enumerate(FOLDS[rank])], local_sem=sem.left)
+        left += ENGINES * len(FOLDS[rank])
+
+    if rank >= 1:
+        g.sync.wait_ge(sem.result, ENGINES)
+        g.sync.dma_start(T.y[:], T.gath[0] if rank == 1 else T.land[:]).then_inc(sem.stored, 16)
+        g.sync.wait_ge(sem.stored, 16)
+
+    if left:
+        g.wait_ge(sem.left, left)

from concourse.bass import DstId, RemoteDMATransfer

N = 8
FOLDS = {0: (5, 6, 7), 1: (2, 3, 4)}
ENGINES = 4

SCRATCH = {
    "gath": ("dram", [N - 1, 128, 8], "bfloat16"),
    "land": ("dram", [128, 8], "bfloat16"),
}
SEMAPHORES = ["staged", "gathered", "result", "left", "stored"]


def rank_program(g, core, T, topo):
    rank = T.rank_of(core)
    if rank is None:
        return
    sem = T.sem

    def dst_id(r):
        rid, pid, _se = topo.addr(T.cores[r])
        return DstId(rid=rid, pnc=pid)

    left = 0

    if rank < N - 1:
        g.sync.dma_start(T.gath[rank], T.x[:]).then_inc(sem.staged, 16)
        g.wait_ge(sem.staged, 16)
        takers = [f for f in sorted(FOLDS) if f != rank and max(FOLDS[f]) > rank]
        g.remote_dma_fused([RemoteDMATransfer(
            dst_ids=[dst_id(f) for f in takers], dma_engine_mask=0x000F,
            remote_sem=sem.result if rank == 0 else sem.gathered,
            srcs=[T.gath[rank]], dsts=[T.gath[rank] for _f in takers], alu_op=0)], local_sem=sem.left)
        left += ENGINES

    if rank in FOLDS:
        foreign = max(FOLDS[rank]) - 1
        if rank == 1:
            g.wait_ge(sem.result, ENGINES)
            foreign -= 1
        g.wait_ge(sem.gathered, foreign * ENGINES)
        g.remote_dma_fused([RemoteDMATransfer(
            dst_ids=[dst_id(r)], dma_engine_mask=0x000F << (ENGINES * k), remote_sem=sem.result,
            srcs=[T.gath[i] for i in range(r)], dsts=[T.land[:]], alu_op=2)
            for k, r in enumerate(FOLDS[rank])], local_sem=sem.left)
        left += ENGINES * len(FOLDS[rank])

    if rank >= 1:
        g.sync.wait_ge(sem.result, ENGINES)
        g.sync.dma_start(T.y[:], T.gath[0] if rank == 1 else T.land[:]).then_inc(sem.stored, 16)
        g.sync.wait_ge(sem.stored, 16)

    if left:
        g.wait_ge(sem.left, left)
